import numpy as np
import ml_dtypes


def mxq(x, axis, fmt="e4m3"):
    dtype, down = {"e4m3": (ml_dtypes.float8_e4m3fn, 7), "e5m2": (ml_dtypes.float8_e5m2, 14)}[fmt]
    v = np.moveaxis(np.asarray(x, np.float32).astype(ml_dtypes.bfloat16).astype(np.float64), axis, -1)
    blocks = v.reshape(v.shape[:-1] + (-1, 32))
    amax = np.abs(blocks).max(-1, keepdims=True)
    byte = np.maximum(np.where(amax > 0, np.frexp(amax)[1] - 1 + 127, 0) - down, 1)
    scale = np.exp2(byte - 127.0)
    codes = (blocks / scale).astype(np.float32).astype(dtype).astype(np.float64)
    return np.moveaxis((codes * scale).reshape(v.shape), -1, axis)


WIDE = False


def mx_kscale(k):
    if not WIDE:
        return np.ones(k)
    levels = np.array([10, -10, 5, -5, 0])
    if k % 512:
        return np.exp2(np.random.permutation(np.resize(levels, k // 32))).repeat(32)
    a = np.empty((k // 512, 16))
    for p in range(k // 512):
        a[p, :8] = np.random.permutation(np.resize(levels, 8))
        for g in range(8):
            far = levels[np.abs(levels - a[p, g]) >= 10]
            a[p, g + 8] = far[np.random.randint(len(far))]
    return np.exp2(a.ravel()).repeat(32)


def f64(x):
    return np.asarray(x).astype(np.float64)


def striped(idx):
    return np.tile(np.asarray(idx).reshape(-1, 16).T, (8, 1)).astype(np.uint16)


def unstriped(offs):
    return offs[:16].T.reshape(-1).astype(np.int64)


E2M1 = np.array([0.0, 0.5, 1.0, 1.5, 2.0, 3.0, 4.0, 6.0, -0.0, -0.5, -1.0, -1.5, -2.0, -3.0, -4.0, -6.0])


def pack_weight(w, fmt):
    k, n = w.shape
    w = f64(np.asarray(w, np.float32).astype(ml_dtypes.bfloat16)).reshape(k // 32, 32, n)
    amax = np.abs(w).max(1)
    if fmt == "e4m3":
        byte = np.frexp(amax)[1] - 1 + 127 - 7
    else:
        mant, ex = np.frexp(amax / 6.0)
        byte = np.where(mant > 0.5, ex, ex - 1) + 127
    byte = np.clip(np.where(amax > 0, byte, 1), 1, 254)
    scaled = (w * np.exp2(127.0 - byte)[:, None, :]).reshape(k, n).astype(np.float32)
    by_word = np.ascontiguousarray(scaled.reshape(k // 512, 128, 4, n).transpose(0, 1, 3, 2))
    if fmt == "e4m3":
        words = by_word.astype(ml_dtypes.float8_e4m3fn).view(np.uint8)
    else:
        c = by_word.astype(ml_dtypes.float4_e2m1fn).view(np.uint8) & 0xF
        words = (c[..., 0::2] | (c[..., 1::2] << 4)).reshape(k // 512, 128, 2 * n)
    return np.ascontiguousarray(words), np.ascontiguousarray(byte.astype(np.uint8).reshape(k // 512, 16, n))


def unpack_weight(words, scales, fmt):
    g, _, n = scales.shape
    words = np.ascontiguousarray(words).reshape(g, 128, n, -1)
    if fmt == "e4m3":
        vals = words.view(ml_dtypes.float8_e4m3fn).astype(np.float64)
    else:
        nib = np.empty((g, 128, n, 4), np.uint8)
        nib[..., 0::2] = words & 0xF
        nib[..., 1::2] = words >> 4
        vals = E2M1[nib]
    vals = vals * np.repeat(np.exp2(scales.astype(np.float64) - 127.0), 8, axis=1)[..., None]
    return vals.transpose(0, 1, 3, 2).reshape(g * 512, n)


D, R, T, I, Q = 512, 512, 2048, 512, 256


def setup_inputs():
    n = np.random.standard_normal
    idx = np.random.permutation(T)[:I]
    fd = mx_kscale(D)
    fr = mx_kscale(R)
    latp = pack_weight(n((R, T)) / fr[:, None], "e4m3")
    return {
        "query": (n((D, Q)) * 0.8 / np.sqrt(D) * fd[:, None]).astype(np.float32),
        "up": (n((R, D)) * 0.5 / np.sqrt(R) * fr[:, None] / fd).astype(np.float32),
        "lat_words": latp[0],
        "lat_scales": latp[1],
        "keys": (n((D, T)) / fd[:, None]).astype(np.float32),
        "offs": striped(idx),
    }


def reference(query, up, lat_words, lat_scales, keys, offs):
    idx = unstriped(offs)
    latu = unpack_weight(lat_words, lat_scales, "e4m3")
    upq = mxq(f64(up), 0, "e4m3")
    latidxg = latu[:, idx]
    z = upq.T @ latidxg
    km = z + f64(keys)[:, idx]
    queryq = mxq(f64(query), 0, "e4m3")
    kmq = mxq(km, 0, "e4m3")
    a = queryq.T @ kmq
    p = np.exp(a - np.max(a, axis=1, keepdims=True))
    y = p / np.sum(p, axis=1, keepdims=True) * 512.0
    return y

@@ -1,0 +1,167 @@
+from contextlib import ExitStack
+
+import concourse.mybir as mybir
+
+D, R, T, I, Q = 512, 512, 2048, 512, 256
+FLOPS = 2 * R * D * I + 2 * D * Q * I
+
+F32 = mybir.dt.float32
+BF16 = mybir.dt.bfloat16
+I32 = mybir.dt.int32
+U32 = mybir.dt.uint32
+U16 = mybir.dt.uint16
+U8 = mybir.dt.uint8
+FP8X4 = mybir.dt.float8_e4m3fn_x4
+ALU = mybir.AluOpType
+EXP = mybir.ActivationFunctionType.Exp
+
+P = 128
+PACK = 4
+HALF = I // 2
+LIST_COLS = HALF // 16
+
+
+def tile_attend_lowrankdelta_kernel(tc, query, up, lat_words, lat_scales, keys, offs, out):
+    nc = tc.nc
+    with ExitStack() as ctx:
+        sb = ctx.enter_context(tc.tile_pool(name="sb", bufs=1))
+        ps = ctx.enter_context(tc.psum_pool(name="ps", bufs=1))
+
+        offsets = sb.tile([P, I // 16], U16, name="offsets")
+        nc.sync.dma_start(offsets[:], offs)
+
+        pool_scales = sb.tile([P, T], U8, name="pool_scales", align_bytes=64)
+        nc.vector.memset(pool_scales[:].bitcast(I32), 0)
+
+        up_raw = sb.tile([P, PACK, D], F32, name="up_raw")
+        up_rows = up.rearrange("(p j) d -> p j d", j=PACK)
+        for j in (0, 2):
+            nc.sync.dma_start(up_raw[:, j : j + 2, :], up_rows[:, j : j + 2, :])
+        query_raw = sb.tile([P, PACK, Q], F32, name="query_raw")
+        nc.sync.dma_start(query_raw[:], query.rearrange("(p j) q -> p j q", j=PACK))
+        for quad in range(4):
+            nc.sync.dma_start(
+                pool_scales[32 * quad : 32 * quad + 4, :].bitcast(I32),
+                lat_scales[0, 4 * quad : 4 * quad + 4, :].bitcast(I32),
+            )
+        pool_words = sb.tile([P, T], U32, name="pool_words", align_bytes=64)
+        nc.sync.dma_start(pool_words[:].bitcast(I32), lat_words[0].rearrange("p t r -> p (t r)").bitcast(I32))
+
+        key_rows = keys.rearrange("(p j) t -> j p t", j=PACK)
+        key_planes = [sb.tile([P, T], F32, name="keys%d" % j, align_bytes=64) for j in range(PACK)]
+        for j in range(PACK):
+            nc.sync.dma_start(key_planes[j][:], key_rows[j])
+
+        up_bf = sb.tile([P, D * PACK], BF16, name="up_bf", align_bytes=64)
+        nc.vector.tensor_copy(
+            up_bf[:].rearrange("p (t m j) -> p m j t", t=PACK, j=PACK),
+            up_raw[:].rearrange("p j (m t) -> p m j t", t=PACK),
+        )
+        query_bf = sb.tile([P, Q * PACK], BF16, name="query_bf", align_bytes=64)
+        nc.scalar.copy(
+            query_bf[:].rearrange("p (c n j) -> p c j n", n=4, j=PACK),
+            query_raw[:].rearrange("p j (c n) -> p c j n", n=4),
+        )
+        query_codes = sb.tile([P, Q], U32, name="query_codes", align_bytes=64)
+        query_scale = sb.tile([P, Q], U8, name="query_scale", align_bytes=64)
+
+        lat_scale = sb.tile([P, I], U8, name="lat_scale", align_bytes=64)
+        nc.vector.tensor_copy(lat_scale[:], pool_scales[:].indirect(offsets[:]))
+
+        up_codes = sb.tile([P, D], U32, name="up_codes", align_bytes=64)
+        up_scale = sb.tile([P, D], U8, name="up_scale", align_bytes=64)
+        nc.vector.quantize_mx(out=up_codes[:].bitcast(FP8X4), scales=up_scale[:], in_=up_bf[:])
+
+        lat_codes = sb.tile([P, I], U32, name="lat_codes", align_bytes=64)
+        nc.vector.tensor_copy(lat_codes[:], pool_words[:].indirect(offsets[:]))
+
+        nc.vector.quantize_mx(out=query_codes[:].bitcast(FP8X4), scales=query_scale[:], in_=query_bf[:])
+
+        z_planes = []
+        for j in range(PACK):
+            cols = slice(P * j, P * (j + 1))
+            z_bank = ps.tile([P, I], F32, name="z_bank%d" % j)
+            nc.tensor.matmul_mx(
+                out=z_bank[:],
+                lhsT=up_codes[:, cols].bitcast(FP8X4),
+                lhsT_scale=up_scale[:, cols],
+                rhs=lat_codes[:].bitcast(FP8X4),
+                rhs_scale=lat_scale[:],
+                start=True,
+                stop=True,
+            )
+            z_plane = sb.tile([P, I], F32, name="z_plane%d" % j)
+            nc.scalar.copy(z_plane[:], z_bank[:])
+            z_planes.append(z_plane)
+
+        km_low = sb.tile([P, 2, I], F32, name="km_low")
+        for j in (0, 1):
+            nc.vector.tensor_tensor(km_low[:, j, :], key_planes[j][:].indirect(offsets[:]), z_planes[j][:], ALU.add)
+        km_bf = [sb.tile([P, HALF, PACK], BF16, name="km_bf%d" % h, align_bytes=64) for h in range(2)]
+        for h in range(2):
+            nc.scalar.copy(
+                km_bf[h][:, :, 0:2],
+                km_low[:, :, HALF * h : HALF * (h + 1)].rearrange("p j i -> p i j"),
+            )
+
+        km_high = [sb.tile([P, 2, HALF], F32, name="km_high%d" % h) for h in range(2)]
+
+        def gather_high(j, h):
+            nc.vector.tensor_tensor(
+                km_high[h][:, j - 2, :],
+                key_planes[j][:].indirect(offsets[:, LIST_COLS * h : LIST_COLS * (h + 1)]),
+                z_planes[j][:, HALF * h : HALF * (h + 1)],
+                ALU.add,
+            )
+
+        for h in range(2):
+            gather_high(2, h)
+        for h in range(2):
+            gather_high(3, h)
+        nc.scalar.copy(km_bf[0][:, :, 2:4], km_high[0][:].rearrange("p j i -> p i j"))
+        nc.vector.tensor_copy(km_bf[1][:, :, 2:4], km_high[1][:].rearrange("p j i -> p i j"))
+
+        scores = {}
+        for h in range(2):
+            km_codes = sb.tile([P, HALF], U32, name="km_codes%d" % h, align_bytes=64)
+            km_scale = sb.tile([P, HALF], U8, name="km_scale%d" % h, align_bytes=64)
+            nc.vector.quantize_mx(
+                out=km_codes[:].bitcast(FP8X4), scales=km_scale[:], in_=km_bf[h][:].rearrange("p i j -> p (i j)")
+            )
+            for b in range(2):
+                rows = slice(P * b, P * (b + 1))
+                bank = ps.tile([P, HALF], F32, name="score_bank%d%d" % (h, b))
+                nc.tensor.matmul_mx(
+                    out=bank[:],
+                    lhsT=query_codes[:, rows].bitcast(FP8X4),
+                    lhsT_scale=query_scale[:, rows],
+                    rhs=km_codes[:].bitcast(FP8X4),
+                    rhs_scale=km_scale[:],
+                    start=True,
+                    stop=True,
+                )
+                scores[h, b] = bank
+
+        negated = [sb.tile([P, I], F32, name="negated%d" % b) for b in range(2)]
+        least = {}
+        for h in range(2):
+            for b in range(2):
+                least[h, b] = sb.tile([P, 1], F32, name="least%d%d" % (h, b))
+                nc.vector.tensor_scalar(
+                    negated[b][:, HALF * h : HALF * (h + 1)],
+                    scores[h, b][:],
+                    -1.0,
+                    least[0, b][:] if h else None,
+                    ALU.mult,
+                    ALU.min,
+                    accum_out=least[h, b][:],
+                )
+        for b in range(2):
+            p = sb.tile([P, I], F32, name="p%d" % b)
+            total = sb.tile([P, 1], F32, name="total%d" % b)
+            nc.scalar.activation(p[:], negated[b][:], EXP, bias=least[1, b][:], scale=-1.0, accum_out=total[:])
+            inverse = sb.tile([P, 1], F32, name="inverse%d" % b)
+            nc.vector.reciprocal(inverse[:], total[:])
+            y = sb.tile([P, I], F32, name="y%d" % b)
+            nc.vector.tensor_scalar(y[:], p[:], inverse[:], 512.0, ALU.mult, ALU.mult)
+            nc.sync.dma_start(out[P * b : P * (b + 1), :], y[:])

@@ -18,7 +18,7 @@ EXP = mybir.ActivationFunctionType.Exp
 P = 128
 PACK = 4
 HALF = I // 2
-LIST_COLS = HALF // 16
+RUNS = ((0, 128), (128, 256), (256, 512))
 
 
 def tile_attend_lowrankdelta_kernel(tc, query, up, lat_words, lat_scales, keys, offs, out):
@@ -35,47 +35,34 @@ def tile_attend_lowrankdelta_kernel(tc, query, up, lat_words, lat_scales, keys, 
 
         up_raw = sb.tile([P, PACK, D], F32, name="up_raw")
         up_rows = up.rearrange("(p j) d -> p j d", j=PACK)
-        for j in (0, 2):
-            nc.sync.dma_start(up_raw[:, j : j + 2, :], up_rows[:, j : j + 2, :])
-        query_raw = sb.tile([P, PACK, Q], F32, name="query_raw")
-        nc.sync.dma_start(query_raw[:], query.rearrange("(p j) q -> p j q", j=PACK))
-        for quad in range(4):
-            nc.sync.dma_start(
-                pool_scales[32 * quad : 32 * quad + 4, :].bitcast(I32),
-                lat_scales[0, 4 * quad : 4 * quad + 4, :].bitcast(I32),
-            )
+        nc.sync.dma_start(up_raw[:, 0:2, :], up_rows[:, 0:2, :])
+        scale_rows = lat_scales[0].rearrange("(quad r) t -> r quad t", r=4)
+        for r in range(4):
+            nc.sync.dma_start(pool_scales[r:P:32, :].bitcast(I32), scale_rows[r].bitcast(I32))
+        nc.sync.dma_start(up_raw[:, 2:4, :], up_rows[:, 2:4, :])
         pool_words = sb.tile([P, T], U32, name="pool_words", align_bytes=64)
         nc.sync.dma_start(pool_words[:].bitcast(I32), lat_words[0].rearrange("p t r -> p (t r)").bitcast(I32))
-
         key_rows = keys.rearrange("(p j) t -> j p t", j=PACK)
         key_planes = [sb.tile([P, T], F32, name="keys%d" % j, align_bytes=64) for j in range(PACK)]
         for j in range(PACK):
             nc.sync.dma_start(key_planes[j][:], key_rows[j])
+        query_raw = sb.tile([P, PACK, Q], F32, name="query_raw")
+        nc.sync.dma_start(query_raw[:], query.rearrange("(p j) q -> p j q", j=PACK))
+
+        lat_scale = sb.tile([P, I], U8, name="lat_scale", align_bytes=64)
+        nc.vector.tensor_copy(lat_scale[:], pool_scales[:].indirect(offsets[:]))
 
         up_bf = sb.tile([P, D * PACK], BF16, name="up_bf", align_bytes=64)
         nc.vector.tensor_copy(
             up_bf[:].rearrange("p (t m j) -> p m j t", t=PACK, j=PACK),
             up_raw[:].rearrange("p j (m t) -> p m j t", t=PACK),
         )
-        query_bf = sb.tile([P, Q * PACK], BF16, name="query_bf", align_bytes=64)
-        nc.scalar.copy(
-            query_bf[:].rearrange("p (c n j) -> p c j n", n=4, j=PACK),
-            query_raw[:].rearrange("p j (c n) -> p c j n", n=4),
-        )
-        query_codes = sb.tile([P, Q], U32, name="query_codes", align_bytes=64)
-        query_scale = sb.tile([P, Q], U8, name="query_scale", align_bytes=64)
-
-        lat_scale = sb.tile([P, I], U8, name="lat_scale", align_bytes=64)
-        nc.vector.tensor_copy(lat_scale[:], pool_scales[:].indirect(offsets[:]))
-
         up_codes = sb.tile([P, D], U32, name="up_codes", align_bytes=64)
         up_scale = sb.tile([P, D], U8, name="up_scale", align_bytes=64)
         nc.vector.quantize_mx(out=up_codes[:].bitcast(FP8X4), scales=up_scale[:], in_=up_bf[:])
 
         lat_codes = sb.tile([P, I], U32, name="lat_codes", align_bytes=64)
         nc.vector.tensor_copy(lat_codes[:], pool_words[:].indirect(offsets[:]))
-
-        nc.vector.quantize_mx(out=query_codes[:].bitcast(FP8X4), scales=query_scale[:], in_=query_bf[:])
 
         z_planes = []
         for j in range(PACK):
@@ -104,52 +91,56 @@ def tile_attend_lowrankdelta_kernel(tc, query, up, lat_words, lat_scales, keys, 
                 km_low[:, :, HALF * h : HALF * (h + 1)].rearrange("p j i -> p i j"),
             )
 
-        km_high = [sb.tile([P, 2, HALF], F32, name="km_high%d" % h) for h in range(2)]
-
-        def gather_high(j, h):
-            nc.vector.tensor_tensor(
-                km_high[h][:, j - 2, :],
-                key_planes[j][:].indirect(offsets[:, LIST_COLS * h : LIST_COLS * (h + 1)]),
-                z_planes[j][:, HALF * h : HALF * (h + 1)],
-                ALU.add,
-            )
-
-        for h in range(2):
-            gather_high(2, h)
-        for h in range(2):
-            gather_high(3, h)
-        nc.scalar.copy(km_bf[0][:, :, 2:4], km_high[0][:].rearrange("p j i -> p i j"))
-        nc.vector.tensor_copy(km_bf[1][:, :, 2:4], km_high[1][:].rearrange("p j i -> p i j"))
-
-        scores = {}
-        for h in range(2):
-            km_codes = sb.tile([P, HALF], U32, name="km_codes%d" % h, align_bytes=64)
-            km_scale = sb.tile([P, HALF], U8, name="km_scale%d" % h, align_bytes=64)
-            nc.vector.quantize_mx(
-                out=km_codes[:].bitcast(FP8X4), scales=km_scale[:], in_=km_bf[h][:].rearrange("p i j -> p (i j)")
-            )
-            for b in range(2):
-                rows = slice(P * b, P * (b + 1))
-                bank = ps.tile([P, HALF], F32, name="score_bank%d%d" % (h, b))
-                nc.tensor.matmul_mx(
-                    out=bank[:],
-                    lhsT=query_codes[:, rows].bitcast(FP8X4),
-                    lhsT_scale=query_scale[:, rows],
-                    rhs=km_codes[:].bitcast(FP8X4),
-                    rhs_scale=km_scale[:],
-                    start=True,
-                    stop=True,
+        km_high = [sb.tile([P, 2, last - first], F32, name="km_high%d" % first) for first, last in RUNS]
+        for j in (2, 3):
+            for run, (first, last) in enumerate(RUNS):
+                nc.vector.tensor_tensor(
+                    km_high[run][:, j - 2, :],
+                    key_planes[j][:].indirect(offsets[:, first // 16 : last // 16]),
+                    z_planes[j][:, first:last],
+                    ALU.add,
                 )
-                scores[h, b] = bank
+        for run in (0, 1):
+            first, last = RUNS[run]
+            nc.scalar.copy(km_bf[0][:, first:last, 2:4], km_high[run][:].rearrange("p j i -> p i j"))
+        nc.vector.tensor_copy(km_bf[1][:, :, 2:4], km_high[2][:].rearrange("p j i -> p i j"))
+
+        query_bf = [sb.tile([P, P * PACK], BF16, name="query_bf%d" % b, align_bytes=64) for b in range(2)]
+        for b in range(2):
+            nc.scalar.copy(
+                query_bf[b][:].rearrange("p (c n j) -> p c j n", n=4, j=PACK),
+                query_raw[:, :, P * b : P * (b + 1)].rearrange("p j (c n) -> p c j n", n=4),
+            )
+
+        km_codes, km_scale, query_codes, query_scale = [], [], [], []
+        for h in range(2):
+            km_codes.append(sb.tile([P, HALF], U32, name="km_codes%d" % h, align_bytes=64))
+            km_scale.append(sb.tile([P, HALF], U8, name="km_scale%d" % h, align_bytes=64))
+            nc.vector.quantize_mx(
+                out=km_codes[h][:].bitcast(FP8X4), scales=km_scale[h][:], in_=km_bf[h][:].rearrange("p i j -> p (i j)")
+            )
+            query_codes.append(sb.tile([P, P], U32, name="query_codes%d" % h, align_bytes=64))
+            query_scale.append(sb.tile([P, P], U8, name="query_scale%d" % h, align_bytes=64))
+            nc.vector.quantize_mx(out=query_codes[h][:].bitcast(FP8X4), scales=query_scale[h][:], in_=query_bf[h][:])
 
         negated = [sb.tile([P, I], F32, name="negated%d" % b) for b in range(2)]
         least = {}
-        for h in range(2):
-            for b in range(2):
+        for b in range(2):
+            for h in range(2):
+                bank = ps.tile([P, HALF], F32, name="score_bank%d%d" % (h, b))
+                nc.tensor.matmul_mx(
+                    out=bank[:],
+                    lhsT=query_codes[b][:].bitcast(FP8X4),
+                    lhsT_scale=query_scale[b][:],
+                    rhs=km_codes[h][:].bitcast(FP8X4),
+                    rhs_scale=km_scale[h][:],
+                    start=True,
+                    stop=True,
+                )
                 least[h, b] = sb.tile([P, 1], F32, name="least%d%d" % (h, b))
                 nc.vector.tensor_scalar(
                     negated[b][:, HALF * h : HALF * (h + 1)],
-                    scores[h, b][:],
+                    bank[:],
                     -1.0,
                     least[0, b][:] if h else None,
                     ALU.mult,

@@ -13,12 +13,13 @@ U16 = mybir.dt.uint16
 U8 = mybir.dt.uint8
 FP8X4 = mybir.dt.float8_e4m3fn_x4
 ALU = mybir.AluOpType
+AXIS_X = mybir.AxisListType.X
 EXP = mybir.ActivationFunctionType.Exp
 
 P = 128
 PACK = 4
 HALF = I // 2
-RUNS = ((0, 128), (128, 256), (256, 512))
+RUNS = ((0, 128), (128, 256), (256, 384), (384, 512))
 
 
 def tile_attend_lowrankdelta_kernel(tc, query, up, lat_words, lat_scales, keys, offs, out):
@@ -27,19 +28,16 @@ def tile_attend_lowrankdelta_kernel(tc, query, up, lat_words, lat_scales, keys, 
         sb = ctx.enter_context(tc.tile_pool(name="sb", bufs=1))
         ps = ctx.enter_context(tc.psum_pool(name="ps", bufs=1))
 
-        offsets = sb.tile([P, I // 16], U16, name="offsets")
-        nc.sync.dma_start(offsets[:], offs)
-
         pool_scales = sb.tile([P, T], U8, name="pool_scales", align_bytes=64)
         nc.vector.memset(pool_scales[:].bitcast(I32), 0)
 
         up_raw = sb.tile([P, PACK, D], F32, name="up_raw")
-        up_rows = up.rearrange("(p j) d -> p j d", j=PACK)
-        nc.sync.dma_start(up_raw[:, 0:2, :], up_rows[:, 0:2, :])
+        nc.sync.dma_start(up_raw[:], up.rearrange("(p j) d -> p j d", j=PACK))
+        offsets = sb.tile([P, I // 16], U16, name="offsets")
+        nc.sync.dma_start(offsets[:], offs)
         scale_rows = lat_scales[0].rearrange("(quad r) t -> r quad t", r=4)
         for r in range(4):
             nc.sync.dma_start(pool_scales[r:P:32, :].bitcast(I32), scale_rows[r].bitcast(I32))
-        nc.sync.dma_start(up_raw[:, 2:4, :], up_rows[:, 2:4, :])
         pool_words = sb.tile([P, T], U32, name="pool_words", align_bytes=64)
         nc.sync.dma_start(pool_words[:].bitcast(I32), lat_words[0].rearrange("p t r -> p (t r)").bitcast(I32))
         key_rows = keys.rearrange("(p j) t -> j p t", j=PACK)
@@ -84,12 +82,12 @@ def tile_attend_lowrankdelta_kernel(tc, query, up, lat_words, lat_scales, keys, 
         km_low = sb.tile([P, 2, I], F32, name="km_low")
         for j in (0, 1):
             nc.vector.tensor_tensor(km_low[:, j, :], key_planes[j][:].indirect(offsets[:]), z_planes[j][:], ALU.add)
-        km_bf = [sb.tile([P, HALF, PACK], BF16, name="km_bf%d" % h, align_bytes=64) for h in range(2)]
-        for h in range(2):
-            nc.scalar.copy(
-                km_bf[h][:, :, 0:2],
-                km_low[:, :, HALF * h : HALF * (h + 1)].rearrange("p j i -> p i j"),
-            )
+        early_bf = sb.tile([P, HALF, PACK], BF16, name="early_bf", align_bytes=64)
+        late_bf = [sb.tile([P, 2 * P, PACK], BF16, name="late_bf%d" % b, align_bytes=64) for b in range(2)]
+        nc.scalar.copy(early_bf[:, :, 0:2], km_low[:, :, 0:HALF].rearrange("p j i -> p i j"))
+        for b in range(2):
+            first = HALF + P * b
+            nc.scalar.copy(late_bf[b][:, 0:P, 0:2], km_low[:, :, first : first + P].rearrange("p j i -> p i j"))
 
         km_high = [sb.tile([P, 2, last - first], F32, name="km_high%d" % first) for first, last in RUNS]
         for j in (2, 3):
@@ -102,57 +100,44 @@ def tile_attend_lowrankdelta_kernel(tc, query, up, lat_words, lat_scales, keys, 
                 )
         for run in (0, 1):
             first, last = RUNS[run]
-            nc.scalar.copy(km_bf[0][:, first:last, 2:4], km_high[run][:].rearrange("p j i -> p i j"))
-        nc.vector.tensor_copy(km_bf[1][:, :, 2:4], km_high[2][:].rearrange("p j i -> p i j"))
-
-        query_bf = [sb.tile([P, P * PACK], BF16, name="query_bf%d" % b, align_bytes=64) for b in range(2)]
+            nc.scalar.copy(early_bf[:, first:last, 2:4], km_high[run][:].rearrange("p j i -> p i j"))
+        for b in range(2):
+            nc.vector.tensor_copy(late_bf[b][:, 0:P, 2:4], km_high[2 + b][:].rearrange("p j i -> p i j"))
         for b in range(2):
             nc.scalar.copy(
-                query_bf[b][:].rearrange("p (c n j) -> p c j n", n=4, j=PACK),
+                late_bf[b][:, P : 2 * P, :].rearrange("p (c n) j -> p c j n", n=4),
                 query_raw[:, :, P * b : P * (b + 1)].rearrange("p j (c n) -> p c j n", n=4),
             )
 
-        km_codes, km_scale, query_codes, query_scale = [], [], [], []
-        for h in range(2):
-            km_codes.append(sb.tile([P, HALF], U32, name="km_codes%d" % h, align_bytes=64))
-            km_scale.append(sb.tile([P, HALF], U8, name="km_scale%d" % h, align_bytes=64))
+        codes, scale = [], []
+        for n, staged in enumerate([early_bf] + late_bf):
+            codes.append(sb.tile([P, HALF], U32, name="codes%d" % n, align_bytes=64))
+            scale.append(sb.tile([P, HALF], U8, name="scale%d" % n, align_bytes=64))
             nc.vector.quantize_mx(
-                out=km_codes[h][:].bitcast(FP8X4), scales=km_scale[h][:], in_=km_bf[h][:].rearrange("p i j -> p (i j)")
+                out=codes[n][:].bitcast(FP8X4), scales=scale[n][:], in_=staged[:].rearrange("p i j -> p (i j)")
             )
-            query_codes.append(sb.tile([P, P], U32, name="query_codes%d" % h, align_bytes=64))
-            query_scale.append(sb.tile([P, P], U8, name="query_scale%d" % h, align_bytes=64))
-            nc.vector.quantize_mx(out=query_codes[h][:].bitcast(FP8X4), scales=query_scale[h][:], in_=query_bf[h][:])
 
-        negated = [sb.tile([P, I], F32, name="negated%d" % b) for b in range(2)]
-        least = {}
         for b in range(2):
-            for h in range(2):
-                bank = ps.tile([P, HALF], F32, name="score_bank%d%d" % (h, b))
+            bank = ps.tile([P, I], F32, name="score_bank%d" % b)
+            for n, first, width in ((0, 0, HALF), (1, HALF, P), (2, HALF + P, P)):
                 nc.tensor.matmul_mx(
-                    out=bank[:],
-                    lhsT=query_codes[b][:].bitcast(FP8X4),
-                    lhsT_scale=query_scale[b][:],
-                    rhs=km_codes[h][:].bitcast(FP8X4),
-                    rhs_scale=km_scale[h][:],
+                    out=bank[:, first : first + width],
+                    lhsT=codes[1 + b][:, P : 2 * P].bitcast(FP8X4),
+                    lhsT_scale=scale[1 + b][:, P : 2 * P],
+                    rhs=codes[n][:, 0:width].bitcast(FP8X4),
+                    rhs_scale=scale[n][:, 0:width],
                     start=True,
                     stop=True,
                 )
-                least[h, b] = sb.tile([P, 1], F32, name="least%d%d" % (h, b))
-                nc.vector.tensor_scalar(
-                    negated[b][:, HALF * h : HALF * (h + 1)],
-                    bank[:],
-                    -1.0,
-                    least[0, b][:] if h else None,
-                    ALU.mult,
-                    ALU.min,
-                    accum_out=least[h, b][:],
-                )
-        for b in range(2):
+            minus_max = sb.tile([P, 1], F32, name="minus_max%d" % b)
+            nc.vector.tensor_reduce(minus_max[:], bank[:], AXIS_X, ALU.max, negate=True)
             p = sb.tile([P, I], F32, name="p%d" % b)
             total = sb.tile([P, 1], F32, name="total%d" % b)
-            nc.scalar.activation(p[:], negated[b][:], EXP, bias=least[1, b][:], scale=-1.0, accum_out=total[:])
+            nc.scalar.activation(p[:], bank[:], EXP, bias=minus_max[:], accum_out=total[:])
             inverse = sb.tile([P, 1], F32, name="inverse%d" % b)
             nc.vector.reciprocal(inverse[:], total[:])
-            y = sb.tile([P, I], F32, name="y%d" % b)
-            nc.vector.tensor_scalar(y[:], p[:], inverse[:], 512.0, ALU.mult, ALU.mult)
-            nc.sync.dma_start(out[P * b : P * (b + 1), :], y[:])
+            for h in range(2):
+                cols = slice(HALF * h, HALF * (h + 1))
+                y = sb.tile([P, HALF], F32, name="y%d%d" % (b, h))
+                nc.vector.tensor_scalar(y[:], p[:, cols], inverse[:], 512.0, ALU.mult, ALU.mult)
+                nc.sync.dma_start(out[P * b : P * (b + 1), cols], y[:])

@@ -98,9 +98,8 @@ def tile_attend_lowrankdelta_kernel(tc, query, up, lat_words, lat_scales, keys, 
                     z_planes[j][:, first:last],
                     ALU.add,
                 )
-        for run in (0, 1):
-            first, last = RUNS[run]
-            nc.scalar.copy(early_bf[:, first:last, 2:4], km_high[run][:].rearrange("p j i -> p i j"))
+        nc.scalar.copy(early_bf[:, 0:P, 2:4], km_high[0][:].rearrange("p j i -> p i j"))
+        nc.vector.tensor_copy(early_bf[:, P:HALF, 2:4], km_high[1][:].rearrange("p j i -> p i j"))
         for b in range(2):
             nc.vector.tensor_copy(late_bf[b][:, 0:P, 2:4], km_high[2 + b][:].rearrange("p j i -> p i j"))
         for b in range(2):

from contextlib import ExitStack

import concourse.mybir as mybir

D, R, T, I, Q = 512, 512, 2048, 512, 256
FLOPS = 2 * R * D * I + 2 * D * Q * I

F32 = mybir.dt.float32
BF16 = mybir.dt.bfloat16
I32 = mybir.dt.int32
U32 = mybir.dt.uint32
U16 = mybir.dt.uint16
U8 = mybir.dt.uint8
FP8X4 = mybir.dt.float8_e4m3fn_x4
ALU = mybir.AluOpType
AXIS_X = mybir.AxisListType.X
EXP = mybir.ActivationFunctionType.Exp

P = 128
PACK = 4
HALF = I // 2
RUNS = ((0, 128), (128, 256), (256, 384), (384, 512))


def tile_attend_lowrankdelta_kernel(tc, query, up, lat_words, lat_scales, keys, offs, out):
    nc = tc.nc
    with ExitStack() as ctx:
        sb = ctx.enter_context(tc.tile_pool(name="sb", bufs=1))
        ps = ctx.enter_context(tc.psum_pool(name="ps", bufs=1))

        pool_scales = sb.tile([P, T], U8, name="pool_scales", align_bytes=64)
        nc.vector.memset(pool_scales[:].bitcast(I32), 0)

        up_raw = sb.tile([P, PACK, D], F32, name="up_raw")
        nc.sync.dma_start(up_raw[:], up.rearrange("(p j) d -> p j d", j=PACK))
        offsets = sb.tile([P, I // 16], U16, name="offsets")
        nc.sync.dma_start(offsets[:], offs)
        scale_rows = lat_scales[0].rearrange("(quad r) t -> r quad t", r=4)
        for r in range(4):
            nc.sync.dma_start(pool_scales[r:P:32, :].bitcast(I32), scale_rows[r].bitcast(I32))
        pool_words = sb.tile([P, T], U32, name="pool_words", align_bytes=64)
        nc.sync.dma_start(pool_words[:].bitcast(I32), lat_words[0].rearrange("p t r -> p (t r)").bitcast(I32))
        key_rows = keys.rearrange("(p j) t -> j p t", j=PACK)
        key_planes = [sb.tile([P, T], F32, name="keys%d" % j, align_bytes=64) for j in range(PACK)]
        for j in range(PACK):
            nc.sync.dma_start(key_planes[j][:], key_rows[j])
        query_raw = sb.tile([P, PACK, Q], F32, name="query_raw")
        nc.sync.dma_start(query_raw[:], query.rearrange("(p j) q -> p j q", j=PACK))

        lat_scale = sb.tile([P, I], U8, name="lat_scale", align_bytes=64)
        nc.vector.tensor_copy(lat_scale[:], pool_scales[:].indirect(offsets[:]))

        up_bf = sb.tile([P, D * PACK], BF16, name="up_bf", align_bytes=64)
        nc.vector.tensor_copy(
            up_bf[:].rearrange("p (t m j) -> p m j t", t=PACK, j=PACK),
            up_raw[:].rearrange("p j (m t) -> p m j t", t=PACK),
        )
        up_codes = sb.tile([P, D], U32, name="up_codes", align_bytes=64)
        up_scale = sb.tile([P, D], U8, name="up_scale", align_bytes=64)
        nc.vector.quantize_mx(out=up_codes[:].bitcast(FP8X4), scales=up_scale[:], in_=up_bf[:])

        lat_codes = sb.tile([P, I], U32, name="lat_codes", align_bytes=64)
        nc.vector.tensor_copy(lat_codes[:], pool_words[:].indirect(offsets[:]))

        z_planes = []
        for j in range(PACK):
            cols = slice(P * j, P * (j + 1))
            z_bank = ps.tile([P, I], F32, name="z_bank%d" % j)
            nc.tensor.matmul_mx(
                out=z_bank[:],
                lhsT=up_codes[:, cols].bitcast(FP8X4),
                lhsT_scale=up_scale[:, cols],
                rhs=lat_codes[:].bitcast(FP8X4),
                rhs_scale=lat_scale[:],
                start=True,
                stop=True,
            )
            z_plane = sb.tile([P, I], F32, name="z_plane%d" % j)
            nc.scalar.copy(z_plane[:], z_bank[:])
            z_planes.append(z_plane)

        km_low = sb.tile([P, 2, I], F32, name="km_low")
        for j in (0, 1):
            nc.vector.tensor_tensor(km_low[:, j, :], key_planes[j][:].indirect(offsets[:]), z_planes[j][:], ALU.add)
        early_bf = sb.tile([P, HALF, PACK], BF16, name="early_bf", align_bytes=64)
        late_bf = [sb.tile([P, 2 * P, PACK], BF16, name="late_bf%d" % b, align_bytes=64) for b in range(2)]
        nc.scalar.copy(early_bf[:, :, 0:2], km_low[:, :, 0:HALF].rearrange("p j i -> p i j"))
        for b in range(2):
            first = HALF + P * b
            nc.scalar.copy(late_bf[b][:, 0:P, 0:2], km_low[:, :, first : first + P].rearrange("p j i -> p i j"))

        km_high = [sb.tile([P, 2, last - first], F32, name="km_high%d" % first) for first, last in RUNS]
        for j in (2, 3):
            for run, (first, last) in enumerate(RUNS):
                nc.vector.tensor_tensor(
                    km_high[run][:, j - 2, :],
                    key_planes[j][:].indirect(offsets[:, first // 16 : last // 16]),
                    z_planes[j][:, first:last],
                    ALU.add,
                )
        nc.scalar.copy(early_bf[:, 0:P, 2:4], km_high[0][:].rearrange("p j i -> p i j"))
        nc.vector.tensor_copy(early_bf[:, P:HALF, 2:4], km_high[1][:].rearrange("p j i -> p i j"))
        for b in range(2):
            nc.vector.tensor_copy(late_bf[b][:, 0:P, 2:4], km_high[2 + b][:].rearrange("p j i -> p i j"))
        for b in range(2):
            nc.scalar.copy(
                late_bf[b][:, P : 2 * P, :].rearrange("p (c n) j -> p c j n", n=4),
                query_raw[:, :, P * b : P * (b + 1)].rearrange("p j (c n) -> p c j n", n=4),
            )

        codes, scale = [], []
        for n, staged in enumerate([early_bf] + late_bf):
            codes.append(sb.tile([P, HALF], U32, name="codes%d" % n, align_bytes=64))
            scale.append(sb.tile([P, HALF], U8, name="scale%d" % n, align_bytes=64))
            nc.vector.quantize_mx(
                out=codes[n][:].bitcast(FP8X4), scales=scale[n][:], in_=staged[:].rearrange("p i j -> p (i j)")
            )

        for b in range(2):
            bank = ps.tile([P, I], F32, name="score_bank%d" % b)
            for n, first, width in ((0, 0, HALF), (1, HALF, P), (2, HALF + P, P)):
                nc.tensor.matmul_mx(
                    out=bank[:, first : first + width],
                    lhsT=codes[1 + b][:, P : 2 * P].bitcast(FP8X4),
                    lhsT_scale=scale[1 + b][:, P : 2 * P],
                    rhs=codes[n][:, 0:width].bitcast(FP8X4),
                    rhs_scale=scale[n][:, 0:width],
                    start=True,
                    stop=True,
                )
            minus_max = sb.tile([P, 1], F32, name="minus_max%d" % b)
            nc.vector.tensor_reduce(minus_max[:], bank[:], AXIS_X, ALU.max, negate=True)
            p = sb.tile([P, I], F32, name="p%d" % b)
            total = sb.tile([P, 1], F32, name="total%d" % b)
            nc.scalar.activation(p[:], bank[:], EXP, bias=minus_max[:], accum_out=total[:])
            inverse = sb.tile([P, 1], F32, name="inverse%d" % b)
            nc.vector.reciprocal(inverse[:], total[:])
            for h in range(2):
                cols = slice(HALF * h, HALF * (h + 1))
                y = sb.tile([P, HALF], F32, name="y%d%d" % (b, h))
                nc.vector.tensor_scalar(y[:], p[:, cols], inverse[:], 512.0, ALU.mult, ALU.mult)
                nc.sync.dma_start(out[P * b : P * (b + 1), cols], y[:])
